import numpy as np, ml_dtypes
CORES = [2,7,10,15,18,23,26,31,34,39,42,47,50,55]
N = 14
G1 = [0,2,4,6,8,10,12]
G2 = [1,3,5,7,9,11,13]
def setup_inputs(rng):
    return {"x1": rng.standard_normal((N, 128, 63), dtype=np.float32), "x2": rng.standard_normal((N, 128, 2), dtype=np.float32).astype(ml_dtypes.bfloat16)}
def reference(x1, x2):
    out = {}
    y = np.full((N, 128, 63), np.nan, x1.dtype)
    for i, r in enumerate(G1):
        y[r] = np.concatenate([x1[s][:, 9 * i:9 * i + 9] for s in G1], axis=1)
    out["y1"] = y
    y = np.full((N, 128, 14), np.nan, x2.dtype)
    s = np.concatenate([x2[r] for r in G2], axis=1)
    for r in G2:
        y[r] = s
    out["y2"] = y
    return out

from concourse.bass import DstId, RemoteDMATransfer

SCRATCH = {
    "xs1": ("sbuf", [128, 63], "float32"),
    "land1": ("sbuf", [128, 63], "float32"),
    "xs2": ("sbuf", [128, 2], "bfloat16"),
    "land2": ("sbuf", [128, 14], "bfloat16"),
}
SEMAPHORES = ["loaded", "sent", "arrived", "stored"]


def _hops(topo, a, b):
    ca, cb = topo.chip(a), topo.chip(b)
    return 1 if (topo.mates(ca, cb) or topo.same_plane(ca, cb)) else 2


def _plan1(topo, cores, i):
    others = [j for j in range(len(cores)) if j != i]
    others.sort(key=lambda j: (-_hops(topo, cores[i], cores[j]), (j - i) % len(cores)))
    first = [(j, 0x03 << (2 * k), 2) for k, j in enumerate(others[:4])]
    second = [(j, 0x0F << (4 * k), 4) for k, j in enumerate(others[4:])]
    return [first, second]


def rank_program(g, core, T, topo):
    rank = T.rank_of(core)
    if rank is None:
        return
    G1, G2 = T.tables["G1"], T.tables["G2"]
    S = T.sem

    if rank in G1:
        cores = [T.cores[r] for r in G1]
        i = G1.index(rank)
        own = slice(9 * i, 9 * i + 9)
        g.sync.dma_start(T.xs1[:], T.x1[:]).then_inc(S.loaded, 16)
        g.scalar.dma_start(T.land1[:, own], T.x1[:, own]).then_inc(S.arrived, 16)
        g.wait_ge(S.loaded, 16)
        sent = 0
        for call in _plan1(topo, cores, i):
            trs = []
            for j, mask, n in call:
                rid, pid, _ = topo.addr(cores[j])
                trs.append(RemoteDMATransfer(dst_ids=[DstId(rid=rid, pnc=pid)], dma_engine_mask=mask,
                                             remote_sem=S.arrived, src=T.xs1[:, 9 * j:9 * j + 9], dst=T.land1[:, own]))
                sent += n
            g.remote_dma_fused(trs, local_sem=S.sent)
        expect = 16
        for s in range(len(cores)):
            if s != i:
                for call in _plan1(topo, cores, s):
                    expect += sum(n for j, _, n in call if j == i)
        g.sync.wait_ge(S.arrived, expect)
        g.sync.dma_start(T.y1[:], T.land1[:]).then_inc(S.stored, 16)
        g.wait_ge(S.sent, sent)
        g.sync.wait_ge(S.stored, 16)
    else:
        cores = [T.cores[r] for r in G2]
        i = G2.index(rank)
        own = slice(2 * i, 2 * i + 2)
        g.sync.dma_start(T.xs2[:], T.x2[:]).then_inc(S.loaded, 16)
        g.scalar.dma_start(T.land2[:, own], T.x2[:]).then_inc(S.arrived, 16)
        g.wait_ge(S.loaded, 16)
        others = [j for j in range(len(cores)) if j != i]
        others.sort(key=lambda j: (-_hops(topo, cores[i], cores[j]), (j - i) % len(cores)))
        ids = []
        for j in others:
            rid, pid, _ = topo.addr(cores[j])
            ids.append(DstId(rid=rid, pnc=pid))
        g.remote_dma_fused([RemoteDMATransfer(dst_ids=ids, dma_engine_mask=0xFF, remote_sem=S.arrived,
                                              srcs=[T.xs2[:]], dsts=[T.land2[:, own] for _ in others])],
                           local_sem=S.sent)
        g.sync.wait_ge(S.arrived, 16 + 8 * len(others))
        g.sync.dma_start(T.y2[:], T.land2[:]).then_inc(S.stored, 16)
        g.wait_ge(S.sent, 8)
        g.sync.wait_ge(S.stored, 16)
